import numpy as np
import ml_dtypes


def mxq(x, axis, fmt="e4m3"):
    dtype, down = {"e4m3": (ml_dtypes.float8_e4m3fn, 7), "e5m2": (ml_dtypes.float8_e5m2, 14)}[fmt]
    v = np.moveaxis(np.asarray(x, np.float32).astype(ml_dtypes.bfloat16).astype(np.float64), axis, -1)
    blocks = v.reshape(v.shape[:-1] + (-1, 32))
    amax = np.abs(blocks).max(-1, keepdims=True)
    byte = np.maximum(np.where(amax > 0, np.frexp(amax)[1] - 1 + 127, 0) - down, 1)
    scale = np.exp2(byte - 127.0)
    codes = (blocks / scale).astype(np.float32).astype(dtype).astype(np.float64)
    return np.moveaxis((codes * scale).reshape(v.shape), -1, axis)


WIDE = False


def mx_kscale(k):
    if not WIDE:
        return np.ones(k)
    levels = np.array([30, -30])
    if k % 512:
        return np.exp2(np.random.permutation(np.resize(levels, k // 32))).repeat(32)
    a = np.empty((k // 512, 16))
    for p in range(k // 512):
        a[p, :8] = np.random.permutation(np.resize(levels, 8))
        for g in range(8):
            far = levels[np.abs(levels - a[p, g]) >= 10]
            a[p, g + 8] = far[np.random.randint(len(far))]
    return np.exp2(a.ravel()).repeat(32)


def f64(x):
    return np.asarray(x).astype(np.float64)


def striped(idx):
    return np.tile(np.asarray(idx).reshape(-1, 16).T, (8, 1)).astype(np.uint16)


def unstriped(offs):
    return offs[:16].T.reshape(-1).astype(np.int64)


def bf(x):
    return np.asarray(x, np.float32).astype(ml_dtypes.bfloat16)


def planes(Y):
    r, m = Y.shape
    b = f64(bf(Y)).reshape(r // 32, 32, m)
    amax = np.abs(b).max(1)
    byte = np.clip(np.where(amax > 0, np.frexp(amax)[1] - 1 + 127 - 7, 1), 1, 254)
    codes = (b * np.exp2(127.0 - byte)[:, None, :]).reshape(r, m).astype(np.float32).astype(ml_dtypes.float8_e4m3fn).view(np.uint8)
    words = codes.reshape(r // 512, 128, 4, m).transpose(0, 1, 3, 2)
    return np.ascontiguousarray(words), np.ascontiguousarray(byte.astype(np.uint8).reshape(r // 512, 16, m))


K, J, N, T, V, Q = 512, 512, 256, 1024, 1024, 64


def setup_inputs():
    n = np.random.standard_normal
    idx = np.random.permutation(T)[:J]
    idx2 = np.random.permutation(V)[:J]
    fj = mx_kscale(J)
    return {
        "xf": (n((K, T)) * np.random.uniform(0.4, 1.6, (1, T))).astype(np.float32),
        "ca": (np.random.uniform(0.5, 1.5, (J, 1)) * fj[:, None]).astype(np.float32),
        "gt": (n((N, V)) * np.exp(0.5 * n((1, V)))).astype(np.float32),
        "cb": (np.random.uniform(0.5, 1.5, (J, 1)) / fj[:, None]).astype(np.float32),
        "gk": (np.random.uniform(0.5, 2.0, (K, 1))).astype(np.float32),
        "offs": striped(idx),
        "offs2": striped(idx2),
    }


def reference(xf, ca, gt, cb, gk, offs, offs2):
    idx = unstriped(offs)
    idx2 = unstriped(offs2)
    xj = f64(xf)[:, idx].T
    uj = xj / (np.mean(np.abs(xj), axis=1, keepdims=True) + 0.1) * f64(ca)
    gr1 = f64(gt)[:, idx2].T
    gj = gr1 / (np.max(np.abs(gr1), axis=1, keepdims=True) + 0.2) * f64(cb)
    ujq = mxq(uj, 0, "e5m2")
    gjq = mxq(gj, 0, "e5m2")
    w = ujq.T @ gjq
    wq = w.reshape(K, Q, N // Q).sum(axis=2)
    y = 0.02 * wq * f64(gk)
    words, scales = planes(y)
    return y, words, scales

@@ -1,0 +1,166 @@
+from contextlib import ExitStack
+
+import concourse.mybir as mybir
+from concourse.masks import make_identity
+
+K, J, N, T, V, Q = 512, 512, 256, 1024, 1024, 64
+FLOPS = 2 * J * K * N
+
+F32 = mybir.dt.float32
+BF16 = mybir.dt.bfloat16
+I32 = mybir.dt.int32
+U32 = mybir.dt.uint32
+U16 = mybir.dt.uint16
+U8 = mybir.dt.uint8
+E5M2 = mybir.dt.float8_e5m2_x4
+E4M3 = mybir.dt.float8_e4m3fn_x4
+ACT = mybir.ActivationFunctionType
+ALU = mybir.AluOpType
+AX = mybir.AxisListType
+
+P = 128
+PACK = 4
+X_BLOCKS = K // P
+G_BLOCKS = N // P
+SPLIT = 256
+
+
+def tile_list_moment_sized_sized_sums_pl_kernel(tc, xf, ca, gt, cb, gk, offs, offs2, out_0, out_1, out_2):
+    nc = tc.nc
+    with ExitStack() as ctx:
+        sb = ctx.enter_context(tc.tile_pool(name="sb", bufs=1))
+        ps = ctx.enter_context(tc.psum_pool(name="ps", bufs=1))
+
+        x_list = sb.tile([P, J // 16], U16, name="x_list")
+        g_list = sb.tile([P, J // 16], U16, name="g_list")
+        g_rows = [sb.tile([P, V], F32, name="g_rows%d" % a) for a in range(G_BLOCKS)]
+        x_rows = [sb.tile([P, T], F32, name="x_rows%d" % b) for b in range(X_BLOCKS)]
+        gt_dealt = gt.rearrange("(p a) v -> a p v", a=G_BLOCKS)
+        xf_dealt = xf.rearrange("(p b) t -> b p t", b=X_BLOCKS)
+        nc.sync.dma_start(g_list[:], offs2)
+        for a in range(G_BLOCKS):
+            nc.sync.dma_start(g_rows[a][:], gt_dealt[a])
+        nc.sync.dma_start(x_list[:], offs)
+        for b in range(X_BLOCKS):
+            nc.sync.dma_start(x_rows[b][:], xf_dealt[b])
+
+        ident = sb.tile([P, P], F32, name="ident")
+        make_identity(nc, ident[:])
+        cb_t = sb.tile([P, PACK], F32, name="cb_t")
+        ca_t = sb.tile([P, PACK], F32, name="ca_t")
+        gk_t = sb.tile([P, PACK], F32, name="gk_t")
+        for tile, vec in ((cb_t, cb), (ca_t, ca), (gk_t, gk)):
+            nc.scalar.dma_start(tile[:], vec.rearrange("(p t) o -> p (t o)", t=PACK))
+
+        def gather_and_turn(rows, offsets, name):
+            picked = sb.tile([P, J], F32, name="picked_" + name)
+            cut = SPLIT // 16
+            nc.vector.tensor_copy(picked[:, :SPLIT], rows[:].indirect(offsets[:, :cut]))
+            nc.scalar.activation(picked[:, SPLIT:], rows[:].indirect(offsets[:, cut:]), ACT.Copy)
+            turned = ps.tile([P, PACK, P], F32, name="turned_" + name, tag="bank_" + name)
+            for t in range(PACK):
+                nc.tensor.transpose(turned[:, t, :], picked[:, t::PACK], ident[:])
+            return turned
+
+        def scale_and_round(dst, turned, factor):
+            nc.vector.tensor_tensor(
+                dst,
+                turned[:].rearrange("p t c -> p c t"),
+                factor[:].unsqueeze(1).to_broadcast([P, P, PACK]),
+                ALU.mult,
+            )
+
+        g_abs = sb.tile([P, G_BLOCKS, PACK, P], F32, name="g_abs")
+        g_max = sb.tile([P, G_BLOCKS, PACK], F32, name="g_max")
+        g_turned = []
+        for a in range(G_BLOCKS):
+            turned = gather_and_turn(g_rows[a], g_list, "g%d" % a)
+            g_turned.append(turned)
+            nc.scalar.activation(g_abs[:, a], turned[:], ACT.Abs)
+            nc.vector.tensor_reduce(g_max[:, a, :], g_abs[:, a], AX.X, ALU.max)
+        g_den = sb.tile([P, PACK], F32, name="g_den")
+        g_top = sb.tile([P, PACK], F32, name="g_top")
+        nc.vector.tensor_tensor(g_top[:], g_max[:, 0, :], g_max[:, 1, :], ALU.max)
+        nc.vector.tensor_scalar(g_den[:], g_top[:], 0.2, None, ALU.add)
+        g_inv = sb.tile([P, PACK], F32, name="g_inv")
+        nc.vector.reciprocal(g_inv[:], g_den[:])
+        g_factor = sb.tile([P, PACK], F32, name="g_factor")
+        nc.vector.tensor_tensor(g_factor[:], g_inv[:], cb_t[:], ALU.mult)
+        g_bf = sb.tile([P, N, PACK], BF16, name="g_bf", align_bytes=64)
+        for a in range(G_BLOCKS):
+            scale_and_round(g_bf[:, a * P : (a + 1) * P, :], g_turned[a], g_factor)
+        g_codes = sb.tile([P, N], U32, name="g_codes", align_bytes=64)
+        g_scales = sb.tile([P, N], U8, name="g_scales", align_bytes=64)
+        nc.vector.quantize_mx(g_codes[:].bitcast(E5M2), g_scales[:], g_bf[:].rearrange("p c t -> p (c t)"))
+
+        row_factor = sb.tile([P, PACK], F32, name="row_factor")
+        nc.vector.tensor_scalar(row_factor[:], gk_t[:], 0.02, None, ALU.mult)
+
+        x_part = sb.tile([P, X_BLOCKS, PACK], F32, name="x_part")
+        x_abs = sb.tile([P, PACK, P], BF16, name="x_abs")
+        x_turned = []
+        for b in range(X_BLOCKS):
+            turned = gather_and_turn(x_rows[b], x_list, "x%d" % b)
+            x_turned.append(turned)
+            for t in range(PACK):
+                nc.scalar.activation(
+                    x_abs[:, t, :], turned[:, t, :], ACT.Abs, scale=1.0 / K, accum_out=x_part[:, b, t : t + 1]
+                )
+        last = X_BLOCKS - 1
+        x_early = sb.tile([P, PACK], F32, name="x_early")
+        nc.vector.tensor_reduce(x_early[:], x_part[:, :last, :].rearrange("p b t -> p t b"), AX.X, ALU.add)
+        x_den = sb.tile([P, PACK], F32, name="x_den")
+        nc.vector.scalar_tensor_tensor(x_den[:], x_part[:, last, :], 0.1, x_early[:], ALU.add, ALU.add)
+        x_inv = sb.tile([P, PACK], F32, name="x_inv")
+        nc.vector.reciprocal(x_inv[:], x_den[:])
+        x_factor = sb.tile([P, PACK], F32, name="x_factor")
+        nc.vector.tensor_tensor(x_factor[:], x_inv[:], ca_t[:], ALU.mult)
+
+        halves = sb.tile([P, 2, PACK, Q], F32, name="halves")
+        acc_tags = ["bank_acc0", "bank_acc1", "bank_g0", "bank_g1"]
+        for b in range(X_BLOCKS):
+            u_bf = sb.tile([P, P, PACK], BF16, name="u_bf%d" % b, align_bytes=64)
+            scale_and_round(u_bf[:], x_turned[b], x_factor)
+            u_codes = sb.tile([P, P], U32, name="u_codes%d" % b, align_bytes=64)
+            u_scales = sb.tile([P, P], U8, name="u_scales%d" % b, align_bytes=64)
+            nc.vector.quantize_mx(u_codes[:].bitcast(E5M2), u_scales[:], u_bf[:].rearrange("p c t -> p (c t)"))
+            acc = ps.tile([P, P], F32, name="acc%d" % b, tag=acc_tags[b])
+            for a in range(G_BLOCKS):
+                cols = slice(a * P, (a + 1) * P)
+                nc.tensor.matmul_mx(
+                    acc[:],
+                    lhsT=u_codes[:].bitcast(E5M2),
+                    lhsT_scale=u_scales[:],
+                    rhs=g_codes[:, cols].bitcast(E5M2),
+                    rhs_scale=g_scales[:, cols],
+                    start=(a == 0),
+                    stop=(a == G_BLOCKS - 1),
+                )
+            nc.scalar.activation(
+                halves[:, :, b, :],
+                acc[:].rearrange("p (q r) -> p r q", r=2),
+                ACT.Copy,
+                scale=row_factor[:, b : b + 1],
+            )
+
+        y_bf = sb.tile([P, Q, PACK], BF16, name="y_bf", align_bytes=64)
+        nc.vector.tensor_tensor(
+            y_bf[:].rearrange("p (c i) t -> p c t i", i=4),
+            halves[:, 0].rearrange("p t (c i) -> p c t i", i=4),
+            halves[:, 1].rearrange("p t (c i) -> p c t i", i=4),
+            ALU.add,
+        )
+        y = sb.tile([P, PACK, Q], F32, name="y")
+        nc.vector.tensor_tensor(y[:], halves[:, 0], halves[:, 1], ALU.add)
+        y_codes = sb.tile([P, Q], U32, name="y_codes", align_bytes=64)
+        y_scales = sb.tile([P, Q], U8, name="y_scales", align_bytes=64)
+        nc.vector.quantize_mx(y_codes[:].bitcast(E4M3), y_scales[:], y_bf[:].rearrange("p c t -> p (c t)"))
+
+        nc.scalar.dma_start(out_0.rearrange("(p t) q -> p t q", t=PACK), y[:])
+        nc.sync.dma_start(out_1[0].rearrange("p c r -> p (c r)").bitcast(I32), y_codes[:].bitcast(I32))
+        for quad in range(4):
+            queue = nc.sync if quad < 2 else nc.scalar
+            queue.dma_start(
+                out_2[0, 4 * quad : 4 * quad + 4, :].bitcast(I32),
+                y_scales[32 * quad : 32 * quad + 4, :].bitcast(I32),
+            )

@@ -23,18 +23,21 @@ PACK = 4
 X_BLOCKS = K // P
 G_BLOCKS = N // P
 SPLIT = 256
+SCALAR_BLOCKS = 2
 
 
 def tile_list_moment_sized_sized_sums_pl_kernel(tc, xf, ca, gt, cb, gk, offs, offs2, out_0, out_1, out_2):
     nc = tc.nc
     with ExitStack() as ctx:
+        lists = ctx.enter_context(tc.tile_pool(name="lists", bufs=1))
         sb = ctx.enter_context(tc.tile_pool(name="sb", bufs=1))
+        ring = ctx.enter_context(tc.tile_pool(name="ring", bufs=3))
         ps = ctx.enter_context(tc.psum_pool(name="ps", bufs=1))
 
-        x_list = sb.tile([P, J // 16], U16, name="x_list")
-        g_list = sb.tile([P, J // 16], U16, name="g_list")
+        x_list = lists.tile([P, J // 16], U16, name="x_list")
+        g_list = lists.tile([P, J // 16], U16, name="g_list")
         g_rows = [sb.tile([P, V], F32, name="g_rows%d" % a) for a in range(G_BLOCKS)]
-        x_rows = [sb.tile([P, T], F32, name="x_rows%d" % b) for b in range(X_BLOCKS)]
+        x_rows = [sb.tile([P, T], F32, name="x_rows%d" % b, tag="x_rows%d" % b) for b in range(X_BLOCKS)]
         gt_dealt = gt.rearrange("(p a) v -> a p v", a=G_BLOCKS)
         xf_dealt = xf.rearrange("(p b) t -> b p t", b=X_BLOCKS)
         nc.sync.dma_start(g_list[:], offs2)
@@ -43,45 +46,64 @@ def tile_list_moment_sized_sized_sums_pl_kernel(tc, xf, ca, gt, cb, gk, offs, of
         nc.sync.dma_start(x_list[:], offs)
         for b in range(X_BLOCKS):
             nc.sync.dma_start(x_rows[b][:], xf_dealt[b])
-
-        ident = sb.tile([P, P], F32, name="ident")
-        make_identity(nc, ident[:])
         cb_t = sb.tile([P, PACK], F32, name="cb_t")
         ca_t = sb.tile([P, PACK], F32, name="ca_t")
         gk_t = sb.tile([P, PACK], F32, name="gk_t")
         for tile, vec in ((cb_t, cb), (ca_t, ca), (gk_t, gk)):
-            nc.scalar.dma_start(tile[:], vec.rearrange("(p t) o -> p (t o)", t=PACK))
+            nc.sync.dma_start(tile[:], vec.rearrange("(p t) o -> p (t o)", t=PACK))
 
-        def gather_and_turn(rows, offsets, name):
-            picked = sb.tile([P, J], F32, name="picked_" + name)
-            cut = SPLIT // 16
-            nc.vector.tensor_copy(picked[:, :SPLIT], rows[:].indirect(offsets[:, :cut]))
-            nc.scalar.activation(picked[:, SPLIT:], rows[:].indirect(offsets[:, cut:]), ACT.Copy)
-            turned = ps.tile([P, PACK, P], F32, name="turned_" + name, tag="bank_" + name)
+        warm = sb.tile([P, 2], F32, name="warm")
+        nc.vector.memset(warm[:, 0:1], 0.0)
+        nc.scalar.activation(warm[:, 1:2], warm[:, 0:1], ACT.Abs)
+
+        ident = sb.tile([P, P], F32, name="ident")
+        make_identity(nc, ident[:])
+
+        def gather(rows, offsets):
+            picked = ring.tile([P, J], F32, name="picked")
+            nc.vector.tensor_copy(picked[:, :SPLIT], rows[:].indirect(offsets[:, : SPLIT // 16]))
+            nc.scalar.activation(picked[:, SPLIT:], rows[:].indirect(offsets[:, SPLIT // 16 :]), ACT.Copy)
+            return picked
+
+        def turn(picked, tag):
+            bank = ps.tile([P, PACK, P], F32, name="turned_" + tag, tag=tag)
             for t in range(PACK):
-                nc.tensor.transpose(turned[:, t, :], picked[:, t::PACK], ident[:])
-            return turned
+                nc.tensor.transpose(bank[:, t, :], picked[:, t::PACK], ident[:])
+            return bank
 
-        def scale_and_round(dst, turned, factor):
+        g_abs = sb.tile([P, G_BLOCKS, PACK, P], F32, name="g_abs")
+        g_max = [sb.tile([P, PACK], F32, name="g_max%d" % a) for a in range(G_BLOCKS)]
+        g_turned = []
+        for a in range(G_BLOCKS):
+            g_turned.append(turn(gather(g_rows[a], g_list), "g%d" % a))
+            nc.scalar.activation(g_abs[:, a], g_turned[a][:], ACT.Abs)
+            nc.vector.tensor_reduce(g_max[a][:], g_abs[:, a], AX.X, ALU.max)
+
+        x_abs = sb.tile([P, PACK, P], BF16, name="x_abs")
+        x_part = sb.tile([P, X_BLOCKS, PACK], F32, name="x_part")
+        x_turned = []
+        for b in range(X_BLOCKS):
+            picked = gather(x_rows[b], x_list)
+            bank = turn(picked, "x%d" % b)
+            views = [bank[:, t, :] for t in range(PACK)]
+            x_turned.append((bank, views))
+            for t in range(PACK):
+                nc.scalar.activation(
+                    x_abs[:, t, :], views[t], ACT.Abs, scale=1.0 / K, accum_out=x_part[:, b, t : t + 1]
+                )
+
+        def scale_and_round(dst, bank, factor):
             nc.vector.tensor_tensor(
                 dst,
-                turned[:].rearrange("p t c -> p c t"),
+                bank[:].rearrange("p t c -> p c t"),
                 factor[:].unsqueeze(1).to_broadcast([P, P, PACK]),
                 ALU.mult,
             )
 
-        g_abs = sb.tile([P, G_BLOCKS, PACK, P], F32, name="g_abs")
-        g_max = sb.tile([P, G_BLOCKS, PACK], F32, name="g_max")
-        g_turned = []
-        for a in range(G_BLOCKS):
-            turned = gather_and_turn(g_rows[a], g_list, "g%d" % a)
-            g_turned.append(turned)
-            nc.scalar.activation(g_abs[:, a], turned[:], ACT.Abs)
-            nc.vector.tensor_reduce(g_max[:, a, :], g_abs[:, a], AX.X, ALU.max)
+        g_first = sb.tile([P, PACK], F32, name="g_first")
+        nc.gpsimd.tensor_scalar(g_first[:], g_max[0][:], 1.0, 0.2, ALU.mult, ALU.add)
         g_den = sb.tile([P, PACK], F32, name="g_den")
-        g_top = sb.tile([P, PACK], F32, name="g_top")
-        nc.vector.tensor_tensor(g_top[:], g_max[:, 0, :], g_max[:, 1, :], ALU.max)
-        nc.vector.tensor_scalar(g_den[:], g_top[:], 0.2, None, ALU.add)
+        nc.vector.scalar_tensor_tensor(g_den[:], g_max[1][:], 0.2, g_first[:], ALU.add, ALU.max)
         g_inv = sb.tile([P, PACK], F32, name="g_inv")
         nc.vector.reciprocal(g_inv[:], g_den[:])
         g_factor = sb.tile([P, PACK], F32, name="g_factor")
@@ -93,37 +115,41 @@ def tile_list_moment_sized_sized_sums_pl_kernel(tc, xf, ca, gt, cb, gk, offs, of
         g_scales = sb.tile([P, N], U8, name="g_scales", align_bytes=64)
         nc.vector.quantize_mx(g_codes[:].bitcast(E5M2), g_scales[:], g_bf[:].rearrange("p c t -> p (c t)"))
 
-        row_factor = sb.tile([P, PACK], F32, name="row_factor")
-        nc.vector.tensor_scalar(row_factor[:], gk_t[:], 0.02, None, ALU.mult)
-
-        x_part = sb.tile([P, X_BLOCKS, PACK], F32, name="x_part")
-        x_abs = sb.tile([P, PACK, P], BF16, name="x_abs")
-        x_turned = []
-        for b in range(X_BLOCKS):
-            turned = gather_and_turn(x_rows[b], x_list, "x%d" % b)
-            x_turned.append(turned)
-            for t in range(PACK):
-                nc.scalar.activation(
-                    x_abs[:, t, :], turned[:, t, :], ACT.Abs, scale=1.0 / K, accum_out=x_part[:, b, t : t + 1]
-                )
-        last = X_BLOCKS - 1
-        x_early = sb.tile([P, PACK], F32, name="x_early")
-        nc.vector.tensor_reduce(x_early[:], x_part[:, :last, :].rearrange("p b t -> p t b"), AX.X, ALU.add)
+        x_run = sb.tile([P, X_BLOCKS - 1, PACK], F32, name="x_run")
+        nc.gpsimd.tensor_scalar(x_run[:, 0, :], x_part[:, 0, :], 1.0, 0.1, ALU.mult, ALU.add)
+        for b in range(1, X_BLOCKS - 1):
+            nc.gpsimd.tensor_tensor(x_run[:, b, :], x_run[:, b - 1, :], x_part[:, b, :], ALU.add)
+        row_factor = sb.tile([P, PACK], F32, name="row_factor", tag="x_rows%d" % (X_BLOCKS - 1))
+        nc.gpsimd.tensor_scalar(row_factor[:], gk_t[:], 0.02, 0.0, ALU.mult, ALU.add)
         x_den = sb.tile([P, PACK], F32, name="x_den")
-        nc.vector.scalar_tensor_tensor(x_den[:], x_part[:, last, :], 0.1, x_early[:], ALU.add, ALU.add)
+        nc.vector.tensor_tensor(x_den[:], x_run[:, X_BLOCKS - 2, :], x_part[:, X_BLOCKS - 1, :], ALU.add)
         x_inv = sb.tile([P, PACK], F32, name="x_inv")
         nc.vector.reciprocal(x_inv[:], x_den[:])
         x_factor = sb.tile([P, PACK], F32, name="x_factor")
         nc.vector.tensor_tensor(x_factor[:], x_inv[:], ca_t[:], ALU.mult)
 
-        halves = sb.tile([P, 2, PACK, Q], F32, name="halves")
-        acc_tags = ["bank_acc0", "bank_acc1", "bank_g0", "bank_g1"]
+        u_bf = [sb.tile([P, P, PACK], BF16, name="u_bf%d" % b, align_bytes=64) for b in range(X_BLOCKS)]
         for b in range(X_BLOCKS):
-            u_bf = sb.tile([P, P, PACK], BF16, name="u_bf%d" % b, align_bytes=64)
-            scale_and_round(u_bf[:], x_turned[b], x_factor)
+            bank, views = x_turned[b]
+            if b < X_BLOCKS - SCALAR_BLOCKS:
+                scale_and_round(u_bf[b][:], bank, x_factor)
+            else:
+                rows = sb.tile([P, PACK, P], BF16, name="u_rows%d" % b)
+                for t in range(PACK):
+                    nc.scalar.activation(rows[:, t, :], views[t], ACT.Copy, scale=x_factor[:, t : t + 1])
+                nc.vector.tensor_copy(
+                    u_bf[b][:].rearrange("p (c i) t -> p c t i", i=4),
+                    rows[:].rearrange("p t (c i) -> p c t i", i=4),
+                )
+
+        halves = sb.tile([P, 2, PACK, Q], F32, name="halves")
+        y_bf = sb.tile([P, Q, PACK], BF16, name="y_bf", align_bytes=64)
+        y = sb.tile([P, PACK, Q], F32, name="y")
+        acc_tags = ["g0", "g1", "acc0", "acc1"]
+        for b in range(X_BLOCKS):
             u_codes = sb.tile([P, P], U32, name="u_codes%d" % b, align_bytes=64)
             u_scales = sb.tile([P, P], U8, name="u_scales%d" % b, align_bytes=64)
-            nc.vector.quantize_mx(u_codes[:].bitcast(E5M2), u_scales[:], u_bf[:].rearrange("p c t -> p (c t)"))
+            nc.vector.quantize_mx(u_codes[:].bitcast(E5M2), u_scales[:], u_bf[b][:].rearrange("p c t -> p (c t)"))
             acc = ps.tile([P, P], F32, name="acc%d" % b, tag=acc_tags[b])
             for a in range(G_BLOCKS):
                 cols = slice(a * P, (a + 1) * P)
@@ -142,16 +168,11 @@ def tile_list_moment_sized_sized_sums_pl_kernel(tc, xf, ca, gt, cb, gk, offs, of
                 ACT.Copy,
                 scale=row_factor[:, b : b + 1],
             )
-
-        y_bf = sb.tile([P, Q, PACK], BF16, name="y_bf", align_bytes=64)
-        nc.vector.tensor_tensor(
-            y_bf[:].rearrange("p (c i) t -> p c t i", i=4),
-            halves[:, 0].rearrange("p t (c i) -> p c t i", i=4),
-            halves[:, 1].rearrange("p t (c i) -> p c t i", i=4),
-            ALU.add,
-        )
-        y = sb.tile([P, PACK, Q], F32, name="y")
-        nc.vector.tensor_tensor(y[:], halves[:, 0], halves[:, 1], ALU.add)
+        for ts in (slice(0, 2), slice(2, PACK)):
+            nc.vector.tensor_tensor(
+                y_bf[:, :, ts].rearrange("p q t -> p t q"), halves[:, 0, ts, :], halves[:, 1, ts, :], ALU.add
+            )
+            nc.vector.tensor_tensor(y[:, ts, :], halves[:, 0, ts, :], halves[:, 1, ts, :], ALU.add)
         y_codes = sb.tile([P, Q], U32, name="y_codes", align_bytes=64)
         y_scales = sb.tile([P, Q], U8, name="y_scales", align_bytes=64)
         nc.vector.quantize_mx(y_codes[:].bitcast(E4M3), y_scales[:], y_bf[:].rearrange("p c t -> p (c t)"))

@@ -31,15 +31,17 @@ def tile_list_moment_sized_sized_sums_pl_kernel(tc, xf, ca, gt, cb, gk, offs, of
     with ExitStack() as ctx:
         lists = ctx.enter_context(tc.tile_pool(name="lists", bufs=1))
         sb = ctx.enter_context(tc.tile_pool(name="sb", bufs=1))
-        ring = ctx.enter_context(tc.tile_pool(name="ring", bufs=3))
+        ring = ctx.enter_context(tc.tile_pool(name="ring", bufs=2))
         ps = ctx.enter_context(tc.psum_pool(name="ps", bufs=1))
 
         x_list = lists.tile([P, J // 16], U16, name="x_list")
         g_list = lists.tile([P, J // 16], U16, name="g_list")
         g_rows = [sb.tile([P, V], F32, name="g_rows%d" % a) for a in range(G_BLOCKS)]
-        x_rows = [sb.tile([P, T], F32, name="x_rows%d" % b, tag="x_rows%d" % b) for b in range(X_BLOCKS)]
+        x_rows = [sb.tile([P, T], F32, name="x_rows%d" % b) for b in range(X_BLOCKS)]
         gt_dealt = gt.rearrange("(p a) v -> a p v", a=G_BLOCKS)
         xf_dealt = xf.rearrange("(p b) t -> b p t", b=X_BLOCKS)
+        gk_t = sb.tile([P, PACK], F32, name="gk_t")
+        nc.sync.dma_start(gk_t[:], gk.rearrange("(p t) o -> p (t o)", t=PACK))
         nc.sync.dma_start(g_list[:], offs2)
         for a in range(G_BLOCKS):
             nc.sync.dma_start(g_rows[a][:], gt_dealt[a])
@@ -48,8 +50,7 @@ def tile_list_moment_sized_sized_sums_pl_kernel(tc, xf, ca, gt, cb, gk, offs, of
             nc.sync.dma_start(x_rows[b][:], xf_dealt[b])
         cb_t = sb.tile([P, PACK], F32, name="cb_t")
         ca_t = sb.tile([P, PACK], F32, name="ca_t")
-        gk_t = sb.tile([P, PACK], F32, name="gk_t")
-        for tile, vec in ((cb_t, cb), (ca_t, ca), (gk_t, gk)):
+        for tile, vec in ((cb_t, cb), (ca_t, ca)):
             nc.sync.dma_start(tile[:], vec.rearrange("(p t) o -> p (t o)", t=PACK))
 
         warm = sb.tile([P, 2], F32, name="warm")
@@ -58,9 +59,11 @@ def tile_list_moment_sized_sized_sums_pl_kernel(tc, xf, ca, gt, cb, gk, offs, of
 
         ident = sb.tile([P, P], F32, name="ident")
         make_identity(nc, ident[:])
+        row_factor = sb.tile([P, PACK], F32, name="row_factor")
+        nc.gpsimd.tensor_scalar(row_factor[:], gk_t[:], 0.02, 0.0, ALU.mult, ALU.add)
 
-        def gather(rows, offsets):
-            picked = ring.tile([P, J], F32, name="picked")
+        def gather(rows, offsets, pool=ring):
+            picked = pool.tile([P, J], F32, name="picked")
             nc.vector.tensor_copy(picked[:, :SPLIT], rows[:].indirect(offsets[:, : SPLIT // 16]))
             nc.scalar.activation(picked[:, SPLIT:], rows[:].indirect(offsets[:, SPLIT // 16 :]), ACT.Copy)
             return picked
@@ -71,21 +74,31 @@ def tile_list_moment_sized_sized_sums_pl_kernel(tc, xf, ca, gt, cb, gk, offs, of
                 nc.tensor.transpose(bank[:, t, :], picked[:, t::PACK], ident[:])
             return bank
 
-        g_abs = sb.tile([P, G_BLOCKS, PACK, P], F32, name="g_abs")
-        g_max = [sb.tile([P, PACK], F32, name="g_max%d" % a) for a in range(G_BLOCKS)]
+        g_abs = [sb.tile([P, PACK, P + a], F32, name="g_abs%d" % a) for a in range(G_BLOCKS)]
+        g_top = sb.tile([P, PACK], F32, name="g_top")
         g_turned = []
         for a in range(G_BLOCKS):
-            g_turned.append(turn(gather(g_rows[a], g_list), "g%d" % a))
-            nc.scalar.activation(g_abs[:, a], g_turned[a][:], ACT.Abs)
-            nc.vector.tensor_reduce(g_max[a][:], g_abs[:, a], AX.X, ALU.max)
+            g_turned.append(turn(gather(g_rows[a], g_list, sb if a == 0 else ring), "g%d" % a))
+            nc.scalar.activation(g_abs[a][:, :, :P], g_turned[a][:], ACT.Abs)
+            nc.vector.tensor_reduce(g_abs[1][:, :, P] if a == 0 else g_top[:], g_abs[a][:], AX.X, ALU.max)
 
         x_abs = sb.tile([P, PACK, P], BF16, name="x_abs")
-        x_part = sb.tile([P, X_BLOCKS, PACK], F32, name="x_part")
+        x_part = sb.tile([P, X_BLOCKS + 1, PACK], F32, name="x_part")
+        nc.gpsimd.tensor_scalar(x_part[:, X_BLOCKS, :], ident[:, :PACK], 0.0, 0.1, ALU.mult, ALU.add)
         x_turned = []
         for b in range(X_BLOCKS):
             picked = gather(x_rows[b], x_list)
-            bank = turn(picked, "x%d" % b)
-            views = [bank[:, t, :] for t in range(PACK)]
+            if b < X_BLOCKS - SCALAR_BLOCKS + 1:
+                bank = turn(picked, "x%d" % b)
+                views = [bank[:, t, :] for t in range(PACK)]
+            else:
+                bank = None
+                views = []
+                for h in range(2):
+                    half = ps.tile([P, 2, P], F32, name="turned_half%d" % h)
+                    for e in range(2):
+                        nc.tensor.transpose(half[:, e, :], picked[:, 2 * h + e :: PACK], ident[:])
+                        views.append(half[:, e, :])
             x_turned.append((bank, views))
             for t in range(PACK):
                 nc.scalar.activation(
@@ -100,10 +113,8 @@ def tile_list_moment_sized_sized_sums_pl_kernel(tc, xf, ca, gt, cb, gk, offs, of
                 ALU.mult,
             )
 
-        g_first = sb.tile([P, PACK], F32, name="g_first")
-        nc.gpsimd.tensor_scalar(g_first[:], g_max[0][:], 1.0, 0.2, ALU.mult, ALU.add)
         g_den = sb.tile([P, PACK], F32, name="g_den")
-        nc.vector.scalar_tensor_tensor(g_den[:], g_max[1][:], 0.2, g_first[:], ALU.add, ALU.max)
+        nc.vector.tensor_scalar(g_den[:], g_top[:], 0.2, None, ALU.add)
         g_inv = sb.tile([P, PACK], F32, name="g_inv")
         nc.vector.reciprocal(g_inv[:], g_den[:])
         g_factor = sb.tile([P, PACK], F32, name="g_factor")
@@ -115,14 +126,8 @@ def tile_list_moment_sized_sized_sums_pl_kernel(tc, xf, ca, gt, cb, gk, offs, of
         g_scales = sb.tile([P, N], U8, name="g_scales", align_bytes=64)
         nc.vector.quantize_mx(g_codes[:].bitcast(E5M2), g_scales[:], g_bf[:].rearrange("p c t -> p (c t)"))
 
-        x_run = sb.tile([P, X_BLOCKS - 1, PACK], F32, name="x_run")
-        nc.gpsimd.tensor_scalar(x_run[:, 0, :], x_part[:, 0, :], 1.0, 0.1, ALU.mult, ALU.add)
-        for b in range(1, X_BLOCKS - 1):
-            nc.gpsimd.tensor_tensor(x_run[:, b, :], x_run[:, b - 1, :], x_part[:, b, :], ALU.add)
-        row_factor = sb.tile([P, PACK], F32, name="row_factor", tag="x_rows%d" % (X_BLOCKS - 1))
-        nc.gpsimd.tensor_scalar(row_factor[:], gk_t[:], 0.02, 0.0, ALU.mult, ALU.add)
         x_den = sb.tile([P, PACK], F32, name="x_den")
-        nc.vector.tensor_tensor(x_den[:], x_run[:, X_BLOCKS - 2, :], x_part[:, X_BLOCKS - 1, :], ALU.add)
+        nc.vector.tensor_reduce(x_den[:], x_part[:].rearrange("p b t -> p t b"), AX.X, ALU.add)
         x_inv = sb.tile([P, PACK], F32, name="x_inv")
         nc.vector.reciprocal(x_inv[:], x_den[:])
         x_factor = sb.tile([P, PACK], F32, name="x_factor")
@@ -145,7 +150,7 @@ def tile_list_moment_sized_sized_sums_pl_kernel(tc, xf, ca, gt, cb, gk, offs, of
         halves = sb.tile([P, 2, PACK, Q], F32, name="halves")
         y_bf = sb.tile([P, Q, PACK], BF16, name="y_bf", align_bytes=64)
         y = sb.tile([P, PACK, Q], F32, name="y")
-        acc_tags = ["g0", "g1", "acc0", "acc1"]
+        acc_tags = ["g0", "g1", "acc", "x0"]
         for b in range(X_BLOCKS):
             u_codes = sb.tile([P, P], U32, name="u_codes%d" % b, align_bytes=64)
             u_scales = sb.tile([P, P], U8, name="u_scales%d" % b, align_bytes=64)

@@ -22,35 +22,36 @@ P = 128
 PACK = 4
 X_BLOCKS = K // P
 G_BLOCKS = N // P
+STEPS = G_BLOCKS + X_BLOCKS
+LAG = 2
 SPLIT = 256
-SCALAR_BLOCKS = 2
+VECTOR_BLOCKS = 2
 
 
 def tile_list_moment_sized_sized_sums_pl_kernel(tc, xf, ca, gt, cb, gk, offs, offs2, out_0, out_1, out_2):
     nc = tc.nc
     with ExitStack() as ctx:
         lists = ctx.enter_context(tc.tile_pool(name="lists", bufs=1))
+        win = ctx.enter_context(tc.tile_pool(name="win", bufs=1))
         sb = ctx.enter_context(tc.tile_pool(name="sb", bufs=1))
         ring = ctx.enter_context(tc.tile_pool(name="ring", bufs=2))
         ps = ctx.enter_context(tc.psum_pool(name="ps", bufs=1))
 
         x_list = lists.tile([P, J // 16], U16, name="x_list")
         g_list = lists.tile([P, J // 16], U16, name="g_list")
-        g_rows = [sb.tile([P, V], F32, name="g_rows%d" % a) for a in range(G_BLOCKS)]
-        x_rows = [sb.tile([P, T], F32, name="x_rows%d" % b) for b in range(X_BLOCKS)]
+        windows = [win.tile([P, T], F32, name="window%d" % i, offset=4 * T * i) for i in range(STEPS)]
         gt_dealt = gt.rearrange("(p a) v -> a p v", a=G_BLOCKS)
         xf_dealt = xf.rearrange("(p b) t -> b p t", b=X_BLOCKS)
-        gk_t = sb.tile([P, PACK], F32, name="gk_t")
-        nc.sync.dma_start(gk_t[:], gk.rearrange("(p t) o -> p (t o)", t=PACK))
-        nc.sync.dma_start(g_list[:], offs2)
-        for a in range(G_BLOCKS):
-            nc.sync.dma_start(g_rows[a][:], gt_dealt[a])
-        nc.sync.dma_start(x_list[:], offs)
-        for b in range(X_BLOCKS):
-            nc.sync.dma_start(x_rows[b][:], xf_dealt[b])
         cb_t = sb.tile([P, PACK], F32, name="cb_t")
         ca_t = sb.tile([P, PACK], F32, name="ca_t")
-        for tile, vec in ((cb_t, cb), (ca_t, ca)):
+        gk_t = sb.tile([P, PACK], F32, name="gk_t")
+        nc.sync.dma_start(g_list[:], offs2)
+        for a in range(G_BLOCKS):
+            nc.sync.dma_start(windows[a][:], gt_dealt[a])
+        nc.sync.dma_start(x_list[:], offs)
+        for b in range(X_BLOCKS):
+            nc.sync.dma_start(windows[G_BLOCKS + b][:], xf_dealt[b])
+        for tile, vec in ((cb_t, cb), (ca_t, ca), (gk_t, gk)):
             nc.sync.dma_start(tile[:], vec.rearrange("(p t) o -> p (t o)", t=PACK))
 
         warm = sb.tile([P, 2], F32, name="warm")
@@ -59,51 +60,57 @@ def tile_list_moment_sized_sized_sums_pl_kernel(tc, xf, ca, gt, cb, gk, offs, of
 
         ident = sb.tile([P, P], F32, name="ident")
         make_identity(nc, ident[:])
-        row_factor = sb.tile([P, PACK], F32, name="row_factor")
-        nc.gpsimd.tensor_scalar(row_factor[:], gk_t[:], 0.02, 0.0, ALU.mult, ALU.add)
 
-        def gather(rows, offsets, pool=ring):
-            picked = pool.tile([P, J], F32, name="picked")
-            nc.vector.tensor_copy(picked[:, :SPLIT], rows[:].indirect(offsets[:, : SPLIT // 16]))
-            nc.scalar.activation(picked[:, SPLIT:], rows[:].indirect(offsets[:, SPLIT // 16 :]), ACT.Copy)
-            return picked
-
-        def turn(picked, tag):
-            bank = ps.tile([P, PACK, P], F32, name="turned_" + tag, tag=tag)
-            for t in range(PACK):
-                nc.tensor.transpose(bank[:, t, :], picked[:, t::PACK], ident[:])
-            return bank
+        def behind(i, shape, name, col=0):
+            return win.tile(shape, F32, name=name, offset=4 * (T * i + col))
 
         g_abs = [sb.tile([P, PACK, P + a], F32, name="g_abs%d" % a) for a in range(G_BLOCKS)]
-        g_top = sb.tile([P, PACK], F32, name="g_top")
-        g_turned = []
-        for a in range(G_BLOCKS):
-            g_turned.append(turn(gather(g_rows[a], g_list, sb if a == 0 else ring), "g%d" % a))
-            nc.scalar.activation(g_abs[a][:, :, :P], g_turned[a][:], ACT.Abs)
-            nc.vector.tensor_reduce(g_abs[1][:, :, P] if a == 0 else g_top[:], g_abs[a][:], AX.X, ALU.max)
-
+        g_top = behind(STEPS - 2, [P, PACK], "g_top")
+        x_first = sb.tile([P, PACK], F32, name="x_first")
+        x_part = behind(STEPS - 1, [P, X_BLOCKS, PACK], "x_part")
+        g_inv = behind(STEPS - 1, [P, PACK], "g_inv", N)
+        row_factor = behind(STEPS - 1, [P, PACK], "row_factor", N + 8)
         x_abs = sb.tile([P, PACK, P], BF16, name="x_abs")
-        x_part = sb.tile([P, X_BLOCKS + 1, PACK], F32, name="x_part")
-        nc.gpsimd.tensor_scalar(x_part[:, X_BLOCKS, :], ident[:, :PACK], 0.0, 0.1, ALU.mult, ALU.add)
-        x_turned = []
-        for b in range(X_BLOCKS):
-            picked = gather(x_rows[b], x_list)
-            if b < X_BLOCKS - SCALAR_BLOCKS + 1:
-                bank = turn(picked, "x%d" % b)
-                views = [bank[:, t, :] for t in range(PACK)]
+
+        banks = []
+        slots = []
+
+        def gather_and_turn(i):
+            offsets = g_list if i < G_BLOCKS else x_list
+            picked = (sb if i == 0 else ring).tile([P, J], F32, name="picked")
+            nc.vector.tensor_copy(picked[:, :SPLIT], windows[i][:].indirect(offsets[:, : SPLIT // 16]))
+            nc.scalar.activation(picked[:, SPLIT:], windows[i][:].indirect(offsets[:, SPLIT // 16 :]), ACT.Copy)
+            per_bank = PACK if i < STEPS - 1 else PACK // 2
+            views = []
+            for h in range(PACK // per_bank):
+                bank = ps.tile([P, per_bank, P], F32, name="turned", tag="bank%d" % (i + h))
+                for e in range(per_bank):
+                    nc.tensor.transpose(bank[:, e, :], picked[:, h * per_bank + e :: PACK], ident[:])
+                    views.append(bank[:, e, :])
+            banks.append(bank)
+            slots.append(views)
+
+        def magnitudes(i):
+            if i < G_BLOCKS:
+                nc.scalar.activation(g_abs[i][:, :, :P], banks[i][:], ACT.Abs)
             else:
-                bank = None
-                views = []
-                for h in range(2):
-                    half = ps.tile([P, 2, P], F32, name="turned_half%d" % h)
-                    for e in range(2):
-                        nc.tensor.transpose(half[:, e, :], picked[:, 2 * h + e :: PACK], ident[:])
-                        views.append(half[:, e, :])
-            x_turned.append((bank, views))
-            for t in range(PACK):
-                nc.scalar.activation(
-                    x_abs[:, t, :], views[t], ACT.Abs, scale=1.0 / K, accum_out=x_part[:, b, t : t + 1]
-                )
+                b = i - G_BLOCKS
+                sums = x_first[:] if b == 0 else x_part[:, b, :]
+                for t in range(PACK):
+                    nc.scalar.activation(
+                        x_abs[:, t, :], slots[i][t], ACT.Abs, scale=1.0 / K, accum_out=sums[:, t : t + 1]
+                    )
+
+        for i in range(STEPS):
+            gather_and_turn(i)
+            if i >= LAG:
+                magnitudes(i - LAG)
+            if i == LAG + 1:
+                nc.vector.tensor_reduce(g_abs[1][:, :, P], g_abs[0][:], AX.X, ALU.max)
+            if i == LAG + 2:
+                nc.vector.tensor_reduce(g_top[:], g_abs[1][:], AX.X, ALU.max)
+        for i in range(STEPS - LAG, STEPS):
+            magnitudes(i)
 
         def scale_and_round(dst, bank, factor):
             nc.vector.tensor_tensor(
@@ -115,17 +122,15 @@ def tile_list_moment_sized_sized_sums_pl_kernel(tc, xf, ca, gt, cb, gk, offs, of
 
         g_den = sb.tile([P, PACK], F32, name="g_den")
         nc.vector.tensor_scalar(g_den[:], g_top[:], 0.2, None, ALU.add)
-        g_inv = sb.tile([P, PACK], F32, name="g_inv")
         nc.vector.reciprocal(g_inv[:], g_den[:])
         g_factor = sb.tile([P, PACK], F32, name="g_factor")
         nc.vector.tensor_tensor(g_factor[:], g_inv[:], cb_t[:], ALU.mult)
         g_bf = sb.tile([P, N, PACK], BF16, name="g_bf", align_bytes=64)
         for a in range(G_BLOCKS):
-            scale_and_round(g_bf[:, a * P : (a + 1) * P, :], g_turned[a], g_factor)
-        g_codes = sb.tile([P, N], U32, name="g_codes", align_bytes=64)
-        g_scales = sb.tile([P, N], U8, name="g_scales", align_bytes=64)
-        nc.vector.quantize_mx(g_codes[:].bitcast(E5M2), g_scales[:], g_bf[:].rearrange("p c t -> p (c t)"))
+            scale_and_round(g_bf[:, a * P : (a + 1) * P, :], banks[a], g_factor)
 
+        nc.gpsimd.tensor_scalar(x_part[:, 0, :], x_first[:], 1.0, 0.1, ALU.mult, ALU.add)
+        nc.gpsimd.tensor_scalar(row_factor[:], gk_t[:], 0.02, 0.0, ALU.mult, ALU.add)
         x_den = sb.tile([P, PACK], F32, name="x_den")
         nc.vector.tensor_reduce(x_den[:], x_part[:].rearrange("p b t -> p t b"), AX.X, ALU.add)
         x_inv = sb.tile([P, PACK], F32, name="x_inv")
@@ -133,15 +138,18 @@ def tile_list_moment_sized_sized_sums_pl_kernel(tc, xf, ca, gt, cb, gk, offs, of
         x_factor = sb.tile([P, PACK], F32, name="x_factor")
         nc.vector.tensor_tensor(x_factor[:], x_inv[:], ca_t[:], ALU.mult)
 
+        g_codes = win.tile([P, N], U32, name="g_codes", align_bytes=64, offset=4 * T * (STEPS - 1))
+        g_scales = sb.tile([P, N], U8, name="g_scales", align_bytes=64)
+        nc.vector.quantize_mx(g_codes[:].bitcast(E5M2), g_scales[:], g_bf[:].rearrange("p c t -> p (c t)"))
+
         u_bf = [sb.tile([P, P, PACK], BF16, name="u_bf%d" % b, align_bytes=64) for b in range(X_BLOCKS)]
         for b in range(X_BLOCKS):
-            bank, views = x_turned[b]
-            if b < X_BLOCKS - SCALAR_BLOCKS:
-                scale_and_round(u_bf[b][:], bank, x_factor)
+            if b < VECTOR_BLOCKS:
+                scale_and_round(u_bf[b][:], banks[G_BLOCKS + b], x_factor)
             else:
                 rows = sb.tile([P, PACK, P], BF16, name="u_rows%d" % b)
                 for t in range(PACK):
-                    nc.scalar.activation(rows[:, t, :], views[t], ACT.Copy, scale=x_factor[:, t : t + 1])
+                    nc.scalar.activation(rows[:, t, :], slots[G_BLOCKS + b][t], ACT.Copy, scale=x_factor[:, t : t + 1])
                 nc.vector.tensor_copy(
                     u_bf[b][:].rearrange("p (c i) t -> p c t i", i=4),
                     rows[:].rearrange("p t (c i) -> p c t i", i=4),
@@ -150,12 +158,11 @@ def tile_list_moment_sized_sized_sums_pl_kernel(tc, xf, ca, gt, cb, gk, offs, of
         halves = sb.tile([P, 2, PACK, Q], F32, name="halves")
         y_bf = sb.tile([P, Q, PACK], BF16, name="y_bf", align_bytes=64)
         y = sb.tile([P, PACK, Q], F32, name="y")
-        acc_tags = ["g0", "g1", "acc", "x0"]
         for b in range(X_BLOCKS):
             u_codes = sb.tile([P, P], U32, name="u_codes%d" % b, align_bytes=64)
             u_scales = sb.tile([P, P], U8, name="u_scales%d" % b, align_bytes=64)
             nc.vector.quantize_mx(u_codes[:].bitcast(E5M2), u_scales[:], u_bf[b][:].rearrange("p c t -> p (c t)"))
-            acc = ps.tile([P, P], F32, name="acc%d" % b, tag=acc_tags[b])
+            acc = ps.tile([P, P], F32, name="acc", tag="bank%d" % b)
             for a in range(G_BLOCKS):
                 cols = slice(a * P, (a + 1) * P)
                 nc.tensor.matmul_mx(

from contextlib import ExitStack

import concourse.mybir as mybir
from concourse.masks import make_identity

K, J, N, T, V, Q = 512, 512, 256, 1024, 1024, 64
FLOPS = 2 * J * K * N

F32 = mybir.dt.float32
BF16 = mybir.dt.bfloat16
I32 = mybir.dt.int32
U32 = mybir.dt.uint32
U16 = mybir.dt.uint16
U8 = mybir.dt.uint8
E5M2 = mybir.dt.float8_e5m2_x4
E4M3 = mybir.dt.float8_e4m3fn_x4
ACT = mybir.ActivationFunctionType
ALU = mybir.AluOpType
AX = mybir.AxisListType

P = 128
PACK = 4
X_BLOCKS = K // P
G_BLOCKS = N // P
STEPS = G_BLOCKS + X_BLOCKS
LAG = 2
SPLIT = 256
VECTOR_BLOCKS = 2


def tile_list_moment_sized_sized_sums_pl_kernel(tc, xf, ca, gt, cb, gk, offs, offs2, out_0, out_1, out_2):
    nc = tc.nc
    with ExitStack() as ctx:
        lists = ctx.enter_context(tc.tile_pool(name="lists", bufs=1))
        win = ctx.enter_context(tc.tile_pool(name="win", bufs=1))
        sb = ctx.enter_context(tc.tile_pool(name="sb", bufs=1))
        ring = ctx.enter_context(tc.tile_pool(name="ring", bufs=2))
        ps = ctx.enter_context(tc.psum_pool(name="ps", bufs=1))

        x_list = lists.tile([P, J // 16], U16, name="x_list")
        g_list = lists.tile([P, J // 16], U16, name="g_list")
        windows = [win.tile([P, T], F32, name="window%d" % i, offset=4 * T * i) for i in range(STEPS)]
        gt_dealt = gt.rearrange("(p a) v -> a p v", a=G_BLOCKS)
        xf_dealt = xf.rearrange("(p b) t -> b p t", b=X_BLOCKS)
        cb_t = sb.tile([P, PACK], F32, name="cb_t")
        ca_t = sb.tile([P, PACK], F32, name="ca_t")
        gk_t = sb.tile([P, PACK], F32, name="gk_t")
        nc.sync.dma_start(g_list[:], offs2)
        for a in range(G_BLOCKS):
            nc.sync.dma_start(windows[a][:], gt_dealt[a])
        nc.sync.dma_start(x_list[:], offs)
        for b in range(X_BLOCKS):
            nc.sync.dma_start(windows[G_BLOCKS + b][:], xf_dealt[b])
        for tile, vec in ((cb_t, cb), (ca_t, ca), (gk_t, gk)):
            nc.sync.dma_start(tile[:], vec.rearrange("(p t) o -> p (t o)", t=PACK))

        warm = sb.tile([P, 2], F32, name="warm")
        nc.vector.memset(warm[:, 0:1], 0.0)
        nc.scalar.activation(warm[:, 1:2], warm[:, 0:1], ACT.Abs)

        ident = sb.tile([P, P], F32, name="ident")
        make_identity(nc, ident[:])

        def behind(i, shape, name, col=0):
            return win.tile(shape, F32, name=name, offset=4 * (T * i + col))

        g_abs = [sb.tile([P, PACK, P + a], F32, name="g_abs%d" % a) for a in range(G_BLOCKS)]
        g_top = behind(STEPS - 2, [P, PACK], "g_top")
        x_first = sb.tile([P, PACK], F32, name="x_first")
        x_part = behind(STEPS - 1, [P, X_BLOCKS, PACK], "x_part")
        g_inv = behind(STEPS - 1, [P, PACK], "g_inv", N)
        row_factor = behind(STEPS - 1, [P, PACK], "row_factor", N + 8)
        x_abs = sb.tile([P, PACK, P], BF16, name="x_abs")

        banks = []
        slots = []

        def gather_and_turn(i):
            offsets = g_list if i < G_BLOCKS else x_list
            picked = (sb if i == 0 else ring).tile([P, J], F32, name="picked")
            nc.vector.tensor_copy(picked[:, :SPLIT], windows[i][:].indirect(offsets[:, : SPLIT // 16]))
            nc.scalar.activation(picked[:, SPLIT:], windows[i][:].indirect(offsets[:, SPLIT // 16 :]), ACT.Copy)
            per_bank = PACK if i < STEPS - 1 else PACK // 2
            views = []
            for h in range(PACK // per_bank):
                bank = ps.tile([P, per_bank, P], F32, name="turned", tag="bank%d" % (i + h))
                for e in range(per_bank):
                    nc.tensor.transpose(bank[:, e, :], picked[:, h * per_bank + e :: PACK], ident[:])
                    views.append(bank[:, e, :])
            banks.append(bank)
            slots.append(views)

        def magnitudes(i):
            if i < G_BLOCKS:
                nc.scalar.activation(g_abs[i][:, :, :P], banks[i][:], ACT.Abs)
            else:
                b = i - G_BLOCKS
                sums = x_first[:] if b == 0 else x_part[:, b, :]
                for t in range(PACK):
                    nc.scalar.activation(
                        x_abs[:, t, :], slots[i][t], ACT.Abs, scale=1.0 / K, accum_out=sums[:, t : t + 1]
                    )

        for i in range(STEPS):
            gather_and_turn(i)
            if i >= LAG:
                magnitudes(i - LAG)
            if i == LAG + 1:
                nc.vector.tensor_reduce(g_abs[1][:, :, P], g_abs[0][:], AX.X, ALU.max)
            if i == LAG + 2:
                nc.vector.tensor_reduce(g_top[:], g_abs[1][:], AX.X, ALU.max)
        for i in range(STEPS - LAG, STEPS):
            magnitudes(i)

        def scale_and_round(dst, bank, factor):
            nc.vector.tensor_tensor(
                dst,
                bank[:].rearrange("p t c -> p c t"),
                factor[:].unsqueeze(1).to_broadcast([P, P, PACK]),
                ALU.mult,
            )

        g_den = sb.tile([P, PACK], F32, name="g_den")
        nc.vector.tensor_scalar(g_den[:], g_top[:], 0.2, None, ALU.add)
        nc.vector.reciprocal(g_inv[:], g_den[:])
        g_factor = sb.tile([P, PACK], F32, name="g_factor")
        nc.vector.tensor_tensor(g_factor[:], g_inv[:], cb_t[:], ALU.mult)
        g_bf = sb.tile([P, N, PACK], BF16, name="g_bf", align_bytes=64)
        for a in range(G_BLOCKS):
            scale_and_round(g_bf[:, a * P : (a + 1) * P, :], banks[a], g_factor)

        nc.gpsimd.tensor_scalar(x_part[:, 0, :], x_first[:], 1.0, 0.1, ALU.mult, ALU.add)
        nc.gpsimd.tensor_scalar(row_factor[:], gk_t[:], 0.02, 0.0, ALU.mult, ALU.add)
        x_den = sb.tile([P, PACK], F32, name="x_den")
        nc.vector.tensor_reduce(x_den[:], x_part[:].rearrange("p b t -> p t b"), AX.X, ALU.add)
        x_inv = sb.tile([P, PACK], F32, name="x_inv")
        nc.vector.reciprocal(x_inv[:], x_den[:])
        x_factor = sb.tile([P, PACK], F32, name="x_factor")
        nc.vector.tensor_tensor(x_factor[:], x_inv[:], ca_t[:], ALU.mult)

        g_codes = win.tile([P, N], U32, name="g_codes", align_bytes=64, offset=4 * T * (STEPS - 1))
        g_scales = sb.tile([P, N], U8, name="g_scales", align_bytes=64)
        nc.vector.quantize_mx(g_codes[:].bitcast(E5M2), g_scales[:], g_bf[:].rearrange("p c t -> p (c t)"))

        u_bf = [sb.tile([P, P, PACK], BF16, name="u_bf%d" % b, align_bytes=64) for b in range(X_BLOCKS)]
        for b in range(X_BLOCKS):
            if b < VECTOR_BLOCKS:
                scale_and_round(u_bf[b][:], banks[G_BLOCKS + b], x_factor)
            else:
                rows = sb.tile([P, PACK, P], BF16, name="u_rows%d" % b)
                for t in range(PACK):
                    nc.scalar.activation(rows[:, t, :], slots[G_BLOCKS + b][t], ACT.Copy, scale=x_factor[:, t : t + 1])
                nc.vector.tensor_copy(
                    u_bf[b][:].rearrange("p (c i) t -> p c t i", i=4),
                    rows[:].rearrange("p t (c i) -> p c t i", i=4),
                )

        halves = sb.tile([P, 2, PACK, Q], F32, name="halves")
        y_bf = sb.tile([P, Q, PACK], BF16, name="y_bf", align_bytes=64)
        y = sb.tile([P, PACK, Q], F32, name="y")
        for b in range(X_BLOCKS):
            u_codes = sb.tile([P, P], U32, name="u_codes%d" % b, align_bytes=64)
            u_scales = sb.tile([P, P], U8, name="u_scales%d" % b, align_bytes=64)
            nc.vector.quantize_mx(u_codes[:].bitcast(E5M2), u_scales[:], u_bf[b][:].rearrange("p c t -> p (c t)"))
            acc = ps.tile([P, P], F32, name="acc", tag="bank%d" % b)
            for a in range(G_BLOCKS):
                cols = slice(a * P, (a + 1) * P)
                nc.tensor.matmul_mx(
                    acc[:],
                    lhsT=u_codes[:].bitcast(E5M2),
                    lhsT_scale=u_scales[:],
                    rhs=g_codes[:, cols].bitcast(E5M2),
                    rhs_scale=g_scales[:, cols],
                    start=(a == 0),
                    stop=(a == G_BLOCKS - 1),
                )
            nc.scalar.activation(
                halves[:, :, b, :],
                acc[:].rearrange("p (q r) -> p r q", r=2),
                ACT.Copy,
                scale=row_factor[:, b : b + 1],
            )
        for ts in (slice(0, 2), slice(2, PACK)):
            nc.vector.tensor_tensor(
                y_bf[:, :, ts].rearrange("p q t -> p t q"), halves[:, 0, ts, :], halves[:, 1, ts, :], ALU.add
            )
            nc.vector.tensor_tensor(y[:, ts, :], halves[:, 0, ts, :], halves[:, 1, ts, :], ALU.add)
        y_codes = sb.tile([P, Q], U32, name="y_codes", align_bytes=64)
        y_scales = sb.tile([P, Q], U8, name="y_scales", align_bytes=64)
        nc.vector.quantize_mx(y_codes[:].bitcast(E4M3), y_scales[:], y_bf[:].rearrange("p c t -> p (c t)"))

        nc.scalar.dma_start(out_0.rearrange("(p t) q -> p t q", t=PACK), y[:])
        nc.sync.dma_start(out_1[0].rearrange("p c r -> p (c r)").bitcast(I32), y_codes[:].bitcast(I32))
        for quad in range(4):
            queue = nc.sync if quad < 2 else nc.scalar
            queue.dma_start(
                out_2[0, 4 * quad : 4 * quad + 4, :].bitcast(I32),
                y_scales[32 * quad : 32 * quad + 4, :].bitcast(I32),
            )
